import numpy as np, ml_dtypes
CORES = [3,7,11,15,131,135,139,143]
N = 8
BF = ml_dtypes.bfloat16
def gentries(a):
    return np.ascontiguousarray(a.reshape(8, 16, -1).transpose(0, 2, 1)).reshape(8, -1)
def gtable(e):
    e = np.asarray(e); return np.ascontiguousarray(e.reshape(8, -1, 16).transpose(0, 2, 1)).reshape(128, -1).astype(np.int32)
V, R, M, RO, P, H, CAP, NEED = 4096, 1280, 2, 2, 4, 3, 96, 9
S, TOP = V // N, 2 ** 20 - 1
def parts(rng):
    base = rng.integers(0, 2 ** 20, (1, 8, 16, 1)); amp = np.exp2(10 + 7 * rng.random((N, 8, 1, R)))
    x = np.clip(base + amp * rng.standard_normal((N, 8, 16, R)), 0, TOP).astype(np.int64)
    t = (np.exp2(14 + 3.5 * rng.random((N, 8, 1, 1))) * (0.5 + rng.random((N, 8, 16, 1)))).astype(np.int64)
    lv = rng.integers(0, V, (N, 8, P, R)); lv = np.where(rng.random((N, 8, 1, R)) < 0.5, np.sort(lv, axis=2), lv)
    cd = rng.integers(0, R, (N, 8, RO, M, V))
    return x, t, lv, cd
def pack(x, t, lv, cd):
    return {"px": np.ascontiguousarray(x.reshape(N, 128, R)).astype(np.int32), "th": np.ascontiguousarray(t.reshape(N, 128, 1)).astype(np.int32),
            "ray": np.stack([gtable(a.reshape(8, -1)) for a in lv]), "cand": np.stack([gtable(a.reshape(8, -1)) for a in cd])}
def setup_inputs(rng):
    return pack(*parts(rng))
def setup_inputs_room(rng):
    x, t, lv, cd = parts(rng); h = R // 8
    t = rng.integers(2 ** 14, 2 ** 15, (N, 8, 16, 1)); x = rng.integers(2 ** 18, 2 ** 19, (1, 8, 16, 1)) + rng.integers(0, 2 ** 13, (N, 8, 16, R))
    inc = np.zeros((8, V), bool); own = np.arange(V) // S
    for o in range(N):
        for g in range(8):
            n = int(rng.choice(np.array([0, 1, CAP - 1, CAP, CAP + 1, S]))); last = o == N - 1 and g < 4
            if o == 0: n = (CAP, CAP + 1, S, CAP - 1, 1, 0, CAP, CAP + 1)[g]
            if last: n = (CAP, 1, CAP - 1, CAP)[g]
            s = rng.permutation(S)[:n]
            if last and not np.any(s == S - 1): s[0] = S - 1
            inc[g, o * S + s] = True
    for a in range(N):
        for g in range(8):
            o = rng.permutation(R); hot, watch, calm = o[:h], o[h:2 * h], o[h:]
            m = np.argsort(rng.random((16, h)), axis=0) < rng.integers(NEED, 17, h)
            x[a, g][:, hot] += m * (rng.choice(np.array([-1, 1]), h) * rng.integers(2 ** 16, 2 ** 17, h))
            lv[a, g, 0, o[:2 * h]] = V - 1; cd[a, g, 0] = rng.choice(calm, (M, V))
            for who, back in ((hot, 1), (watch, 2)):
                v = np.flatnonzero(inc[g] & ((own + back) % N == a))
                cd[a, g, 0, rng.integers(0, M, len(v)), v] = rng.choice(who, len(v))
    return pack(x, t, lv, cd)
def setup_inputs_ties(rng):
    x, t, lv, cd = parts(rng); n = min(R // 8, S)
    base = rng.choice(np.array([0, 2 ** 19, TOP]), 8); base[0] = 0; base[1] = TOP; base[2] = 2 ** 19; sg = np.where(base > 2 ** 19, -1, 1)
    t = rng.choice(np.array([0, 1, 1000, 2 ** 18, 2 ** 19 - 8]), (N, 8, 1, 1)) + rng.integers(0, 3, (N, 8, 16, 1))
    x = np.tile(base.reshape(1, 8, 1, 1), (N, 1, 16, R))
    for a in range(N):
        for g in range(8):
            o = rng.permutation(R); hot, watch, calm = o[:n], o[n:2 * n], o[n:]; b, e = (a - 1) % N, (a - 2) % N
            m = (np.argsort(rng.random((16, n)), axis=0) < rng.choice(np.array([NEED - 1, NEED, 16]), n)).astype(np.int64)
            x[a, g][:, hot] = base[g] + sg[g] * (t[b, g] + m)
            v = b * S + rng.permutation(S)[:n]
            lv[a, g, 0, hot] = np.where(rng.random(n) < 0.4, v, np.where(rng.random(n) < 0.5, V - 1, np.maximum(v - 1, 0)))
            lv[a, g, 0, watch] = V - 1
            cd[a, g, 0] = rng.choice(calm, (M, V)); cd[a, g, 0, 0, v] = hot
            cd[a, g, 0, M - 1, e * S:(e + 1) * S] = rng.choice(watch, S)
    return pack(x, t, lv, cd)
def setup_inputs_alike(rng):
    x, t, lv, cd = parts(rng)
    cd[:, ::4] = rng.choice(np.array([0, R - 1, R // 2, 5]), (N, 2, RO, M, V)); cd[:, 3] = cd[:, 3][:, :, :1]
    lv[:, 1::2] = lv[:, 1::2, :1]
    lv[:, 2] = rng.choice(np.array([0, V - 1]), (N, P, R)); lv[:, 6] = rng.integers(0, 16, (N, P, R))
    return pack(x, t, lv, cd)
def setup_inputs_dim(rng):
    x, t, lv, cd = parts(rng); q = rng.permutation(N); k = int(rng.integers(0, 7)); o = int(q[1])
    lv[:, k] = lv[:, k] // 2; lv[q[0], :7] = rng.integers(0, 4, (7, P, R)); t[o] = TOP; t[q[2]] = 0
    for a, pixel in ((int(q[0]), 0), (int(q[3]), TOP)):
        s = rng.permutation(R)[:R // 16]; x[a, 7][:, s] = pixel; lv[a, 7, 0, s] = V - 1
        cd[a, 7, 0, 0, o * S:(o + 1) * S] = rng.choice(s, S)
    return pack(x, t, lv, cd)
def setup_inputs_spread(rng):
    x, t, lv, cd = parts(rng)
    t = np.minimum(np.exp2(10 + 10 * rng.random((N, 8, 16, 1))).astype(np.int64), TOP)
    x = np.minimum((np.exp2(20 * rng.random((N, 8, 1, R))) * rng.random((N, 8, 16, R))).astype(np.int64), TOP)
    return pack(x, t, lv, cd)
def check_inputs(d):
    bad = []
    for k, lo, hi in (("px", 0, TOP), ("th", 0, TOP), ("ray", 0, V - 1), ("cand", 0, R - 1)):
        if np.min(d[k]) < lo or np.max(d[k]) > hi: bad.append("range of " + k)
    return bad
def reference(px, th, ray, cand):
    x = px.astype(np.int64).reshape(N, 8, 16, R); t = th.astype(np.int64).reshape(N, 8, 16, 1)
    lv = np.stack([gentries(a) for a in ray]).astype(np.int64).reshape(N, 8, P, R)
    cd = np.stack([gentries(a) for a in cand]).astype(np.int64).reshape(N, 8, RO, M, V)
    c = np.zeros((N, 8, R), np.int64); number = np.arange(V)
    for rnd in range(RO):
        w = np.take_along_axis(lv, c[:, :, None, :], 2)[:, :, 0]
        lo = np.full((8, 16, V), TOP + 1, np.int64); hi = np.full((8, 16, V), -1, np.int64)
        for a in range(N):
            for m in range(M):
                ix = cd[a, :, rnd, m]
                sees = (number <= np.take_along_axis(w[a], ix, 1))[:, None, :]
                v = np.take_along_axis(x[a], ix[:, None, :], 2)
                lo = np.minimum(lo, np.where(sees, v, TOP + 1)); hi = np.maximum(hi, np.where(sees, v, -1))
        carved = np.zeros((8, V), bool)
        for o in range(N):
            far = (hi[:, :, o * S:(o + 1) * S] - lo[:, :, o * S:(o + 1) * S] > t[o]).astype(np.int64)
            odd = np.add.reduce(far, axis=1) >= NEED
            carved[:, o * S:(o + 1) * S] = odd & (np.add.accumulate(odd.astype(np.int64), axis=1) <= CAP)
        for step in range(H):
            w = np.take_along_axis(lv, c[:, :, None, :], 2)[:, :, 0]
            nx, nc = [], []
            for a in range(N):
                gone = np.take_along_axis(carved, w[a], 1); e = np.take_along_axis(lo, w[a][:, None, :], 2)
                nx.append(np.where(gone[:, None, :], np.clip(x[a] + ((x[a] - e) >> 2), 0, TOP), x[a]))
                nc.append(np.minimum(c[a] + gone.astype(np.int64), P - 1))
            x = np.stack(nx); c = np.stack(nc)
    yc = np.stack([gtable(c[a]) for a in range(N)])
    return {"yx": x.reshape(N, 128, R).astype(np.float32), "yc": yc.astype(np.float32)}

@@ -1,0 +1,416 @@
+from concourse.bass import DstId, RemoteDMATransfer
+from concourse.mybir import dt, AluOpType, ActivationFunctionType
+
+A = AluOpType
+AF = ActivationFunctionType
+V, R, M, RO, P4, H, CAP, NEED = 4096, 1280, 2, 2, 4, 3, 96, 9
+TOP = 2 ** 20 - 1
+D = float(2 ** 21)
+XW = R + 8
+
+_S = {
+    "ones": ([128, V], "float32"),
+    "cio": ([128, V], "float32"),
+    "wg": ([128, 4 * 2048], "bfloat16"),
+    "lo": ([128, V], "float32"), "hi": ([128, V], "float32"),
+    "bl": ([128, V], "float32"), "bh": ([128, V], "float32"),
+    "xs": ([128, 4 * R], "int32"), "xl": ([128, XW], "float32"), "xh": ([128, XW], "float32"),
+    "wr": ([128, R], "float32"), "fl": ([128, 3 * R], "bfloat16"), "ft": ([128, V], "bfloat16"),
+    "yb": ([128, R], "float32"), "x5": ([128, R], "float32"), "xf": ([128, R], "float32"),
+    "s1": ([128, 1024], "float32"), "s2": ([128, 512], "float32"),
+    "lof": ([128, 512], "float32"), "df": ([128, 512], "float32"), "odd": ([128, 512], "float32"),
+    "pre": ([128, 520], "float32"), "c96": ([128, 512], "float32"),
+    "far": ([128, 512], "bfloat16"), "cv": ([128, 512], "bfloat16"), "fb": ([128, 512], "float32"),
+    "ci0": ([128, 512], "int32"), "ci1": ([128, 512], "int32"),
+    "cf0": ([128, 512], "float32"), "cf1": ([128, 512], "float32"),
+    "cu0": ([128, 512], "uint16"), "cu1": ([128, 512], "uint16"),
+    "off": ([128, 512], "uint16"), "tm": ([128, 512], "float32"),
+    "ri": ([128, 320], "int32"), "rf": ([128, 320], "float32"), "ru": ([128, 320], "uint16"),
+    "rd": ([128, 240], "float32"), "lq": ([128, 240], "uint16"), "lf": ([128, 240], "float32"),
+    "ef": ([128, 240], "float32"), "eg": ([128, 160], "float32"), "t1": ([128, 80], "float32"),
+    "t2": ([128, 80], "float32"), "t3": ([128, 80], "float32"), "t4": ([128, 80], "float32"),
+    "kk": ([128, 80], "float32"), "k2": ([128, 80], "float32"), "so": ([128, 80], "uint16"),
+    "cu": ([128, 80], "float32"), "cn": ([128, 80], "float32"), "rc": ([128, 80], "float32"),
+    "dsel": ([128, 16 * 128], "bfloat16"), "selo": ([128, 8 * 128], "bfloat16"),
+    "bones": ([128, 128], "bfloat16"), "ni": ([128, 128], "bfloat16"), "nv": ([128, 128], "bfloat16"),
+    "eye": ([128, 128], "float32"), "mi": ([128, 128], "int32"), "mj": ([128, 128], "int32"),
+    "mf": ([128, 128], "float32"), "mg": ([128, 128], "float32"),
+    "pi": ([128, 8], "int32"), "pf": ([128, 8], "float32"), "cm": ([128, 16], "float32"), "sm": ([128, 8], "float32"),
+    "thi": ([128, 1], "int32"), "thf": ([128, 1], "float32"),
+}
+SCRATCH = {k: ("sbuf", s, d) for k, (s, d) in _S.items()}
+for _k, _w, _d in (("c0", 64, "int32"), ("r", 40, "int32"), ("p", 160, "int32"), ("c1", 64, "int32"),
+                   ("y", 160, "float32"), ("c", 10, "float32")):
+    SCRATCH["st" + _k] = ("dram", [8, 128, _w], _d)
+    SCRATCH["ld" + _k] = ("dram", [8, 128, _w], _d)
+SCRATCH["stt"] = ("dram", [128, 1], "int32")
+SCRATCH["ldt"] = ("dram", [8, 128, 1], "int32")
+SCRATCH["fd"] = ("dram", [16, V], "float32")
+SCRATCH["pp"] = ("psum", [128, 2048], "float32")
+for _k in range(4):
+    SCRATCH["z%d" % _k] = ("psum", [128, 512], "float32")
+PSUM = ("pp", "z0", "z1", "z2", "z3")
+
+CLASSES = ("c0", "r", "p", "t", "c1", "y", "c")
+TWO_CALLS = ("c0", "p", "c1", "y", "r")
+SEMAPHORES = (["q_v", "q_a", "q_t", "q_g", "sent"] + ["arr_" + k for k in CLASSES] + ["stg_" + k for k in CLASSES]
+              + ["own_" + k for k in CLASSES] + ["get_" + k for k in CLASSES]
+              + ["rl0", "rl1", "rh0", "rh1", "fs0", "fs1", "fg0", "fg1"])
+
+
+def plan(core, cores, topo, two):
+    r = cores.index(core)
+    order = [cores[(r + k) % len(cores)] for k in range(1, len(cores))]
+    near = [d for d in order if d in topo.cores_of(core)]
+    far = [d for d in order if d not in near]
+    fe = topo.engines(core, far[0])
+    ne = [e for e in topo.engines(core, near[0]) if e not in fe]
+    if two:
+        first = [(d, fe[2 * k:2 * k + 2]) for k, d in enumerate(far[:4])]
+        second = [(d, fe[4 * k:4 * k + 4]) for k, d in enumerate(far[4:])]
+        return [second + [(near[0], ne)], first]
+    return [[(d, fe[k:k + 1]) for k, d in enumerate(far)] + [(near[0], ne)]]
+
+
+def rank_program(g, core, T, topo):
+    q = T.rank_of(core)
+    if q is None:
+        return
+    cores = list(T.cores)
+    sem = T.sem
+    queues = {"v": g.vector, "a": g.scalar, "t": g.tensor, "s": g.sync, "g": g}
+    csem = {"v": "q_v", "a": "q_a", "t": "q_t", "g": "q_g"}
+    total = {}
+    known = {}
+    closed = {}
+    hist = {}
+
+    def need(qn, s, val):
+        if val is None:
+            val = total[s]
+            closed[s] = True
+        if known.get((qn, s), 0) < val:
+            queues[qn].wait_ge(sem[s], val)
+            known[(qn, s)] = val
+
+    def depend(qn, acc, own):
+        wants = {}
+        for name, lo, hi, w in acc:
+            ps = name in PSUM
+            if ps:
+                lo, hi = lo // 512 * 512, -(-hi // 512) * 512
+            for (l2, h2, w2, q2, s2, v2) in hist.get(name, []):
+                if l2 >= hi or h2 <= lo or s2 == own:
+                    continue
+                if not (w or w2 or (ps and q2 != qn)):
+                    continue
+                v = total[s2] if v2 is None else v2
+                if v2 is None:
+                    closed[s2] = True
+                wants[s2] = max(wants.get(s2, 0), v)
+        for s in wants:
+            need(qn, s, wants[s])
+
+    def record(qn, acc, s, val):
+        for name, lo, hi, w in acc:
+            if name in PSUM:
+                lo, hi = lo // 512 * 512, -(-hi // 512) * 512
+            h = hist.setdefault(name, [])
+            if w:
+                h[:] = [e for e in h if not (e[0] >= lo and e[1] <= hi and not (e[4] == s and e[5] is None))]
+            h.append((lo, hi, w, qn, s, val))
+
+    def accs(rd, wr):
+        return [(n, a, b, False) for n, a, b in rd] + [(n, a, b, True) for n, a, b in wr]
+
+    def op(qn, rd, wr, fn):
+        s = csem[qn]
+        acc = accs(rd, wr)
+        depend(qn, acc, None)
+        fn(queues[qn]).then_inc(sem[s], 1)
+        total[s] = total.get(s, 0) + 1
+        record(qn, acc, s, total[s])
+
+    def ops(qn, rd, wr, fns):
+        s = csem[qn]
+        acc = accs(rd, wr)
+        depend(qn, acc, None)
+        for f in fns[:-1]:
+            f(queues[qn])
+        fns[-1](queues[qn]).then_inc(sem[s], 1)
+        total[s] = total.get(s, 0) + 1
+        record(qn, acc, s, total[s])
+
+    def dma(qn, s, rd, wr, out, in_):
+        assert s not in closed, s
+        acc = accs(rd, wr)
+        depend(qn, acc, s)
+        queues[qn].dma_start(out=out, in_=in_).then_inc(sem[s], 16)
+        total[s] = total.get(s, 0) + 16
+        record(qn, acc, s, None)
+
+    def send(c, piece):
+        need("g", "stg_" + c, None)
+        for call in plan(core, cores, topo, c in TWO_CALLS):
+            tr = []
+            for d, eng in call:
+                rid, pid = topo.addr(d, core)
+                m = sum(1 << e for e in eng)
+                assert m & topo.mask(core, d) == m
+                tr.append(RemoteDMATransfer(dst_ids=[DstId(rid=rid, pnc=pid)], dma_engine_mask=m,
+                                            remote_sem=sem["arr_" + c], srcs=[piece(T.rank_of(d))], dsts=[T["ld" + c][q]]))
+                total["sent"] = total.get("sent", 0) + len(eng)
+            g.remote_dma_fused(tr, local_sem=sem.sent)
+        n = 0
+        for o in cores:
+            if o != core:
+                for call in plan(o, cores, topo, c in TWO_CALLS):
+                    n += sum(len(eng) for d, eng in call if d == core)
+        total["arr_" + c] = n
+        record("far", [("ld" + c, 0, q, True), ("ld" + c, q + 1, 8, True)], "arr_" + c, n)
+
+    dma("s", "stg_c0", [], [("stc0", 0, 8)], T.stc0[:], T.cand[:, 0:512])
+    dma("a", "stg_r", [], [("str", 0, 8)], T["str"][:], T.ray[:])
+    dma("s", "stg_p", [], [("stp", 0, 8)], T.stp[:], T.px[:])
+    dma("a", "own_c0", [], [("ldc0", q, q + 1)], T.ldc0[q], T.cand[16 * q:16 * q + 16, 0:512])
+    dma("a", "own_r", [], [("ldr", q, q + 1)], T.ldr[q], T.ray[16 * q:16 * q + 16, :])
+    dma("s", "own_p", [], [("ldp", q, q + 1)], T.ldp[q], T.px[16 * q:16 * q + 16, :])
+    dma("a", "stg_c1", [], [("stc1", 0, 8)], T.stc1[:], T.cand[:, 512:1024])
+    dma("s", "own_c1", [], [("ldc1", q, q + 1)], T.ldc1[q], T.cand[16 * q:16 * q + 16, 512:1024])
+    dma("s", "stg_t", [], [("stt", 0, 8)], T.stt[:], T.th[:])
+    dma("s", "own_t", [], [("ldt", q, q + 1)], T.ldt[q], T.th[:])
+    op("g", [], [("pi", 0, 1)], lambda e: e.iota(T.pi[:, 0:1], [[0, 1]], 0, 1))
+    send("r", lambda d: T["str"][d])
+    send("c0", lambda d: T.stc0[d])
+    send("p", lambda d: T.stp[d])
+    send("c1", lambda d: T.stc1[d])
+    send("t", lambda d: T.stt[:])
+    dma("s", "get_r", [("ldr", 0, 8)], [("ri", 0, 320)], T.ri[:], T.ldr[:])
+    dma("s", "get_c0", [("ldc0", 0, 8)], [("ci0", 0, 512)], T.ci0[:], T.ldc0[:])
+    dma("s", "get_p", [("ldp", 0, 8)], [("xs", 0, R)], T.xs[:, 0:R], T.ldp[:])
+    dma("s", "get_c1", [("ldc1", 0, 8)], [("ci1", 0, 512)], T.ci1[:], T.ldc1[:])
+    dma("s", "get_t", [("ldt", 0, 8)], [("thi", 0, 1)], T.thi[:], T.ldt[:, 16 * q:16 * q + 16, :])
+
+    def ap(b):
+        return T[b[0]][:, b[1]:b[2]]
+
+    def ts(out, in0, s1, s2, o0, o1=None, extra=(), qn="v"):
+        if o1 is None:
+            op(qn, [in0] + list(extra), [out], lambda e: e.tensor_scalar(ap(out), ap(in0), s1, None, o0))
+        else:
+            op(qn, [in0] + list(extra), [out], lambda e: e.tensor_scalar(ap(out), ap(in0), s1, s2, o0, o1))
+
+    def tt(out, in0, in1, o):
+        op("v", [in0, in1], [out], lambda e: e.tensor_tensor(ap(out), ap(in0), ap(in1), o))
+
+    def copy(out, in_):
+        op("v", [in_], [out], lambda e: e.tensor_copy(ap(out), ap(in_)))
+
+    def fill(out, c):
+        op("v", [], [out], lambda e: e.memset(ap(out), c))
+
+    def act(out, in_, scale=1.0, bias=0.0):
+        op("a", [in_], [out], lambda e: e.activation(ap(out), ap(in_), AF.Identity, bias=bias, scale=scale))
+
+    def act_gather(out, win, lst, bias=0.0):
+        op("a", [win, lst], [out],
+           lambda e: e.activation(ap(out), ap(win).indirect(ap(lst)), AF.Identity, bias=bias, scale=1.0))
+
+    def tt_gather(out, win, lst, in1, o):
+        op("v", [win, lst, in1], [out], lambda e: e.tensor_tensor(ap(out), ap(win).indirect(ap(lst)), ap(in1), o))
+
+    fill(("ones", 0, V), 1.0)
+    op("v", [("ones", 0, V)], [("cio", 0, V)],
+       lambda e: e.tensor_tensor_scan(T.cio[:], T.ones[:], T.ones[:], -1.0, A.add, A.mult))
+    ts(("pi", 1, 2), ("pi", 0, 1), 15, None, A.bitwise_and)
+    ts(("pi", 2, 3), ("pi", 0, 1), 4, None, A.arith_shift_right)
+    copy(("pf", 0, 3), ("pi", 0, 3))
+    ts(("pf", 3, 4), ("pf", 1, 2), -1.0, 255.0, A.mult, A.add)
+    pcol, c16, bcol, k255 = (T.pf[:, k:k + 1] for k in range(4))
+    pfr = [("pf", 0, 4)]
+    copy(("mi", 0, 128), ("cio", 0, 128))
+    ts(("eye", 0, 128), ("cio", 0, 128), pcol, None, A.is_equal, extra=pfr)
+    ts(("cm", 0, 16), ("cio", 0, 16), c16, -2048.0, A.is_equal, A.mult, extra=pfr)
+    ts(("sm", 0, 8), ("cio", 0, 8), 16.0, pcol, A.mult, A.is_equal, extra=pfr)
+    ts(("rc", 0, 80), ("cio", 0, 80), 16.0, c16, A.mult, A.add, extra=pfr)
+    ts(("mj", 0, 128), ("mi", 0, 128), 31, None, A.bitwise_and)
+    ts(("mi", 0, 128), ("mi", 0, 128), 4, None, A.arith_shift_right)
+    copy(("mf", 0, 128), ("mj", 0, 128))
+    copy(("mg", 0, 128), ("mi", 0, 128))
+    ts(("nv", 0, 128), ("mf", 0, 128), -16.0, k255, A.mult, A.add, extra=pfr)
+    ts(("bones", 0, 128), ("mg", 0, 128), bcol, None, A.is_equal, extra=pfr)
+    ts(("ni", 0, 128), ("eye", 0, 128), -2048.0, None, A.mult)
+    for i in range(16):
+        ts(("dsel", 128 * i, 128 * i + 128), ("eye", 0, 128), T.cm[:, i:i + 1], None, A.mult, extra=[("cm", 0, 16)])
+    for o in range(8):
+        ts(("selo", 128 * o, 128 * o + 128), ("ones", 0, 128), T.sm[:, o:o + 1], None, A.mult, extra=[("sm", 0, 8)])
+    fill(("xl", R, XW), D)
+    fill(("xh", R, XW), -1.0)
+    fill(("c96", 0, 512), float(CAP))
+    fill(("pre", 7, 8), 0.0)
+
+    copy(("ru", 0, 320), ("ri", 0, 320))
+    copy(("rf", 0, 320), ("ri", 0, 320))
+    copy(("cu0", 0, 512), ("ci0", 0, 512))
+    copy(("cf0", 0, 512), ("ci0", 0, 512))
+    tt(("rd", 0, 240), ("rf", 80, 320), ("rf", 0, 240), A.subtract)
+
+    def extract(bank, ncol, buf, base, with_v):
+        fns = []
+        for i in range(16):
+            fns.append(lambda e, i=i: e.matmul(T[bank][:, 0:ncol], T.dsel[:, 128 * i:128 * i + 128],
+                                               T[buf][:, base + i:base + 16 * ncol:16], i == 0, (not with_v) and i == 15))
+        rd = [("dsel", 0, 2048), (buf, base, base + 16 * ncol)]
+        if with_v:
+            fns.append(lambda e: e.matmul(T[bank][:, 0:ncol], T.ni[:], T.nv[:, 0:ncol], False, True))
+            rd += [("ni", 0, 128), ("nv", 0, 128)]
+        ops("t", rd, [(bank, 0, 512)], fns)
+
+    def reduce_ranks(b, o, last):
+        act(("pp", 0, 1024), (b, 0, 1024))
+        act(("pp", 1024, 2048), (b, 1024, 2048))
+        tt(("s1", 0, 1024), ("pp", 0, 1024), (b, 2048, 3072), o)
+        tt(("pp", 0, 1024), ("pp", 1024, 2048), (b, 3072, 4096), o)
+        tt(("s2", 0, 512), ("pp", 0, 512), ("s1", 0, 512), o)
+        tt(("pp", 1024, 1536), ("pp", 512, 1024), ("s1", 512, 1024), o)
+        tt(last, ("pp", 1024, 1536), ("s2", 0, 512), o)
+
+    def relayout(s, b, to, h, split):
+        for k in range(4):
+            o = 4 * h + k
+            for a in range(8):
+                qn = "a" if split and k % 2 else "s"
+                dma(qn, s, [(b, 512 * o, 512 * o + 512)], [(to, 512 * a, 512 * a + 512)],
+                    T[to][16 * o:16 * o + 16, 512 * a:512 * a + 512], T[b][16 * a:16 * a + 16, 512 * o:512 * o + 512])
+
+    for t in range(RO):
+        cu, cf = "cu%d" % t, "cf%d" % t
+        lst = "ru" if t == 0 else "lq"
+        act_gather(("wr", 0, R), ("cio", 0, V), (lst, 0, 80))
+        for h in range(2):
+            for k in range(4):
+                b = 2048 * h + 512 * k
+                c = b // 16
+                j = 2 * h
+                act_gather(("wg", 2048 * j + 512 * k, 2048 * j + 512 * k + 512), ("wr", 0, R), (cu, c, c + 32), -(b + 255.0))
+                j, c = j + 1, c + 256
+                op("v", [("wr", 0, R), (cu, c, c + 32)], [("wg", 2048 * j + 512 * k, 2048 * j + 512 * k + 512)],
+                   lambda e, j=j, c=c, b=b, k=k: e.tensor_scalar(
+                       T.wg[:, 2048 * j + 512 * k:2048 * j + 512 * k + 512],
+                       T.wr[:, 0:R].indirect(T[cu][:, c:c + 32]), b + 255.0, None, A.subtract))
+        for j in range(4):
+            extract("z%d" % j, 128, "wg", 2048 * j, True)
+        if t == 0:
+            copy(("xl", 0, R), ("xs", 0, R))
+        else:
+            copy(("xs", 0, R), ("xl", 0, R))
+
+        def lists(j):
+            h, m = j // 2, j % 2
+            tt(("tm", 128 * j, 128 * j + 128), ("z%d" % j, 0, 128), (cf, 256 * m + 128 * h, 256 * m + 128 * h + 128), A.max)
+            ts(("off", 128 * j, 128 * j + 128), ("tm", 128 * j, 128 * j + 128), float(R), None, A.min)
+
+        def first(b, x, h):
+            act_gather((b, 2048 * h, 2048 * h + 2048), (x, 0, XW), ("off", 256 * h, 256 * h + 128))
+
+        def second(b, x, h, o):
+            tt_gather((b, 2048 * h, 2048 * h + 2048), (x, 0, XW), ("off", 256 * h + 128, 256 * h + 256),
+                      (b, 2048 * h, 2048 * h + 2048), o)
+
+        lists(0)
+        first("lo", "xl", 0)
+        lists(1)
+        lists(2)
+        first("lo", "xl", 1)
+        act(("xh", 0, R), ("xl", 0, R))
+        first("hi", "xh", 0)
+        first("hi", "xh", 1)
+        act(("x5", 0, R), ("xl", 0, R), scale=1.25)
+        second("lo", "xl", 0, A.min)
+        relayout("rl%d" % t, "lo", "bl", 0, False)
+        lists(3)
+        second("lo", "xl", 1, A.min)
+        relayout("rl%d" % t, "lo", "bl", 1, False)
+        second("hi", "xh", 0, A.max)
+        relayout("rh%d" % t, "hi", "bh", 0, False)
+        second("hi", "xh", 1, A.max)
+        reduce_ranks("bl", A.min, ("lof", 0, 512))
+        relayout("rh%d" % t, "hi", "bh", 1, True)
+        act(("fb", 0, 512), ("lof", 0, 512), scale=-0.25, bias=-0.375)
+        for o in range(8):
+            dma("s", "fs%d" % t, [("fb", 0, 512)], [("fd", 512 * o, 512 * o + 512)],
+                T.fd[:, 512 * o:512 * o + 512], T.fb[16 * o:16 * o + 16, :])
+        for a in range(8):
+            dma("s", "fg%d" % t, [("fd", 0, V)], [("ones", 0, V)], T.ones[16 * a:16 * a + 16, :], T.fd[:])
+        if t == 0:
+            copy(("thf", 0, 1), ("thi", 0, 1))
+            copy(("cu1", 0, 512), ("ci1", 0, 512))
+            copy(("cf1", 0, 512), ("ci1", 0, 512))
+        reduce_ranks("bh", A.max, ("pp", 1536, 2048))
+
+        tt(("df", 0, 512), ("pp", 1536, 2048), ("lof", 0, 512), A.subtract)
+        ts(("far", 0, 512), ("df", 0, 512), T.thf[:, 0:1], None, A.is_gt, extra=[("thf", 0, 1)])
+        ops("t", [("bones", 0, 128), ("far", 0, 512)], [("z0", 0, 512)],
+            [lambda e: e.matmul(T.z0[:], T.bones[:], T.far[:], True, True)])
+        ts(("odd", 0, 512), ("z0", 0, 512), float(NEED), None, A.is_ge)
+        op("v", [("odd", 0, 512), ("c96", 0, 512)], [("pre", 8, 520)],
+           lambda e: e.tensor_tensor_scan(T.pre[:, 8:520], T.odd[:], T.c96[:], 0.0, A.add, A.min))
+        tt(("cv", 0, 512), ("pre", 8, 520), ("pre", 7, 519), A.subtract)
+        for o in range(8):
+            z = "z%d" % (o % 4)
+            ops("t", [("selo", 128 * o, 128 * o + 128), ("cv", 0, 512)], [(z, 0, 512)],
+                [lambda e, z=z, o=o: e.matmul(T[z][:], T.selo[:, 128 * o:128 * o + 128], T.cv[:], True, True)])
+            act(("ft", 512 * o, 512 * o + 512), (z, 0, 512))
+
+        for s in range(H):
+            act_gather(("fl", R * s, R * s + R), ("ft", 0, V), (lst, 80 * s, 80 * s + 80))
+            extract("z%d" % s, 80, "fl", R * s, False)
+        for s in range(H):
+            tt_gather(("yb", 0, R), ("ones", 0, V), (lst, 80 * s, 80 * s + 80), ("x5", 0, R), A.add)
+            ts(("xs", R * s + R, R * s + 2 * R), ("yb", 0, R), 0.0, float(TOP), A.max, A.min)
+            if s < H - 1:
+                ts(("x5", 0, R), ("xs", R * s + R, R * s + 2 * R), 1.25, None, A.mult)
+        for s in range(H):
+            ts(("ef", 80 * s, 80 * s + 80), ("z%d" % s, 0, 80), -1024.0, None, A.is_lt)
+        e1, e2, e3 = ("ef", 0, 80), ("eg", 0, 80), ("eg", 80, 160)
+        tt(e2, e1, ("ef", 80, 160), A.mult)
+        tt(e3, e2, ("ef", 160, 240), A.mult)
+        tt(("k2", 0, 80), e1, e2, A.add)
+        if t == 0:
+            tt(("t1", 0, 80), e1, ("rd", 0, 80), A.mult)
+            tt(("t2", 0, 80), e2, ("rd", 80, 160), A.mult)
+            tt(("t3", 0, 80), e3, ("rd", 160, 240), A.mult)
+            tt(("t1", 0, 80), ("t1", 0, 80), ("rf", 0, 80), A.add)
+            tt(("t2", 0, 80), ("t2", 0, 80), ("t3", 0, 80), A.add)
+            tt(("lf", 0, 80), ("t1", 0, 80), ("t2", 0, 80), A.add)
+            copy(("lq", 0, 80), ("lf", 0, 80))
+        tt(("kk", 0, 80), ("k2", 0, 80), e3, A.add)
+        ts(("t4", 0, 80), ("kk", 0, 80), float(R), None, A.mult)
+        tt(("t4", 0, 80), ("t4", 0, 80), ("rc", 0, 80), A.add)
+        copy(("so", 0, 80), ("t4", 0, 80))
+        to = ("xl", 0, R) if t == 0 else ("xf", 0, R)
+        op("v", [("xs", 0, 4 * R), ("so", 0, 80)], [to],
+           lambda e: e.tensor_copy(ap(to), T.xs[:].indirect(T.so[:])))
+        if t == 0:
+            tt(("t1", 0, 80), e1, ("rd", 80, 160), A.mult)
+            tt(("t2", 0, 80), e2, ("rd", 160, 240), A.mult)
+            tt(("t3", 0, 80), e1, ("rd", 160, 240), A.mult)
+            tt(("t1", 0, 80), ("t1", 0, 80), ("rf", 80, 160), A.add)
+            tt(("lf", 80, 160), ("t1", 0, 80), ("t2", 0, 80), A.add)
+            tt(("lf", 160, 240), ("t3", 0, 80), ("rf", 160, 240), A.add)
+            copy(("lq", 80, 240), ("lf", 80, 240))
+            copy(("cu", 0, 80), ("kk", 0, 80))
+        else:
+            tt(("t1", 0, 80), ("cu", 0, 80), ("kk", 0, 80), A.add)
+            ts(("cn", 0, 80), ("t1", 0, 80), 3.0, None, A.min)
+
+    dma("s", "stg_y", [("xf", 0, R)], [("sty", 0, 8)], T.sty[:], T.xf[:])
+    dma("a", "stg_c", [("cn", 0, 80)], [("stc", 0, 8)], T.stc[:], T.cn[:])
+    send("y", lambda d: T.sty[d])
+    send("c", lambda d: T.stc[d])
+    dma("s", "own_y", [("sty", 0, 8)], [("ldy", q, q + 1)], T.ldy[q], T.sty[q])
+    dma("a", "own_c", [("stc", 0, 8)], [("ldc", q, q + 1)], T.ldc[q], T.stc[q])
+    dma("s", "get_y", [("ldy", 0, 8)], [], T.yx[:], T.ldy[:])
+    dma("a", "get_c", [("ldc", 0, 8)], [], T.yc[:], T.ldc[:])
+    for s in total:
+        need("g", s, total[s])

@@ -1,9 +1,9 @@
 from concourse.bass import DstId, RemoteDMATransfer
-from concourse.mybir import dt, AluOpType, ActivationFunctionType
+from concourse.mybir import AluOpType, ActivationFunctionType
 
 A = AluOpType
 AF = ActivationFunctionType
-V, R, M, RO, P4, H, CAP, NEED = 4096, 1280, 2, 2, 4, 3, 96, 9
+V, R, RO, H, CAP, NEED = 4096, 1280, 2, 3, 96, 9
 TOP = 2 ** 20 - 1
 D = float(2 ** 21)
 XW = R + 8
@@ -18,7 +18,7 @@ _S = {
     "wr": ([128, R], "float32"), "fl": ([128, 3 * R], "bfloat16"), "ft": ([128, V], "bfloat16"),
     "yb": ([128, R], "float32"), "x5": ([128, R], "float32"), "xf": ([128, R], "float32"),
     "s1": ([128, 1024], "float32"), "s2": ([128, 512], "float32"),
-    "lof": ([128, 512], "float32"), "df": ([128, 512], "float32"), "odd": ([128, 512], "float32"),
+    "lof": ([128, 512], "float32"), "lt": ([128, 512], "float32"), "odd": ([128, 512], "float32"),
     "pre": ([128, 520], "float32"), "c96": ([128, 512], "float32"),
     "far": ([128, 512], "bfloat16"), "cv": ([128, 512], "bfloat16"), "fb": ([128, 512], "float32"),
     "ci0": ([128, 512], "int32"), "ci1": ([128, 512], "int32"),
@@ -27,7 +27,7 @@ _S = {
     "off": ([128, 512], "uint16"), "tm": ([128, 512], "float32"),
     "ri": ([128, 320], "int32"), "rf": ([128, 320], "float32"), "ru": ([128, 320], "uint16"),
     "rd": ([128, 240], "float32"), "lq": ([128, 240], "uint16"), "lf": ([128, 240], "float32"),
-    "ef": ([128, 240], "float32"), "eg": ([128, 160], "float32"), "t1": ([128, 80], "float32"),
+    "ef": ([128, 240], "float32"), "eg": ([128, 240], "float32"), "t1": ([128, 80], "float32"),
     "t2": ([128, 80], "float32"), "t3": ([128, 80], "float32"), "t4": ([128, 80], "float32"),
     "kk": ([128, 80], "float32"), "k2": ([128, 80], "float32"), "so": ([128, 80], "uint16"),
     "cu": ([128, 80], "float32"), "cn": ([128, 80], "float32"), "rc": ([128, 80], "float32"),
@@ -40,7 +40,7 @@ _S = {
 }
 SCRATCH = {k: ("sbuf", s, d) for k, (s, d) in _S.items()}
 for _k, _w, _d in (("c0", 64, "int32"), ("r", 40, "int32"), ("p", 160, "int32"), ("c1", 64, "int32"),
-                   ("y", 160, "float32"), ("c", 10, "float32")):
+                   ("y0", 80, "float32"), ("y1", 80, "float32"), ("c", 10, "float32")):
     SCRATCH["st" + _k] = ("dram", [8, 128, _w], _d)
     SCRATCH["ld" + _k] = ("dram", [8, 128, _w], _d)
 SCRATCH["stt"] = ("dram", [128, 1], "int32")
@@ -51,8 +51,8 @@ for _k in range(4):
     SCRATCH["z%d" % _k] = ("psum", [128, 512], "float32")
 PSUM = ("pp", "z0", "z1", "z2", "z3")
 
-CLASSES = ("c0", "r", "p", "t", "c1", "y", "c")
-TWO_CALLS = ("c0", "p", "c1", "y", "r")
+CLASSES = ("c0", "r", "p", "t", "c1", "y0", "y1", "c")
+TWO_CALLS = ("c0", "p", "c1", "y0", "y1", "r")
 SEMAPHORES = (["q_v", "q_a", "q_t", "q_g", "sent"] + ["arr_" + k for k in CLASSES] + ["stg_" + k for k in CLASSES]
               + ["own_" + k for k in CLASSES] + ["get_" + k for k in CLASSES]
               + ["rl0", "rl1", "rh0", "rh1", "fs0", "fs1", "fg0", "fg1"])
@@ -123,14 +123,6 @@ def rank_program(g, core, T, topo):
     def accs(rd, wr):
         return [(n, a, b, False) for n, a, b in rd] + [(n, a, b, True) for n, a, b in wr]
 
-    def op(qn, rd, wr, fn):
-        s = csem[qn]
-        acc = accs(rd, wr)
-        depend(qn, acc, None)
-        fn(queues[qn]).then_inc(sem[s], 1)
-        total[s] = total.get(s, 0) + 1
-        record(qn, acc, s, total[s])
-
     def ops(qn, rd, wr, fns):
         s = csem[qn]
         acc = accs(rd, wr)
@@ -140,6 +132,9 @@ def rank_program(g, core, T, topo):
         fns[-1](queues[qn]).then_inc(sem[s], 1)
         total[s] = total.get(s, 0) + 1
         record(qn, acc, s, total[s])
+
+    def op(qn, rd, wr, fn):
+        ops(qn, rd, wr, [fn])
 
     def dma(qn, s, rd, wr, out, in_):
         assert s not in closed, s
@@ -175,30 +170,28 @@ def rank_program(g, core, T, topo):
     dma("a", "own_c0", [], [("ldc0", q, q + 1)], T.ldc0[q], T.cand[16 * q:16 * q + 16, 0:512])
     dma("a", "own_r", [], [("ldr", q, q + 1)], T.ldr[q], T.ray[16 * q:16 * q + 16, :])
     dma("s", "own_p", [], [("ldp", q, q + 1)], T.ldp[q], T.px[16 * q:16 * q + 16, :])
-    dma("a", "stg_c1", [], [("stc1", 0, 8)], T.stc1[:], T.cand[:, 512:1024])
-    dma("s", "own_c1", [], [("ldc1", q, q + 1)], T.ldc1[q], T.cand[16 * q:16 * q + 16, 512:1024])
-    dma("s", "stg_t", [], [("stt", 0, 8)], T.stt[:], T.th[:])
-    dma("s", "own_t", [], [("ldt", q, q + 1)], T.ldt[q], T.th[:])
     op("g", [], [("pi", 0, 1)], lambda e: e.iota(T.pi[:, 0:1], [[0, 1]], 0, 1))
     send("r", lambda d: T["str"][d])
     send("c0", lambda d: T.stc0[d])
     send("p", lambda d: T.stp[d])
-    send("c1", lambda d: T.stc1[d])
-    send("t", lambda d: T.stt[:])
     dma("s", "get_r", [("ldr", 0, 8)], [("ri", 0, 320)], T.ri[:], T.ldr[:])
     dma("s", "get_c0", [("ldc0", 0, 8)], [("ci0", 0, 512)], T.ci0[:], T.ldc0[:])
     dma("s", "get_p", [("ldp", 0, 8)], [("xs", 0, R)], T.xs[:, 0:R], T.ldp[:])
-    dma("s", "get_c1", [("ldc1", 0, 8)], [("ci1", 0, 512)], T.ci1[:], T.ldc1[:])
-    dma("s", "get_t", [("ldt", 0, 8)], [("thi", 0, 1)], T.thi[:], T.ldt[:, 16 * q:16 * q + 16, :])
+    dma("s", "stg_t", [], [("stt", 0, 8)], T.stt[:], T.th[:])
+    dma("s", "own_t", [], [("ldt", q, q + 1)], T.ldt[q], T.th[:])
+    dma("s", "stg_c1", [], [("stc1", 0, 8)], T.stc1[:], T.cand[:, 512:1024])
+    dma("s", "own_c1", [], [("ldc1", q, q + 1)], T.ldc1[q], T.cand[16 * q:16 * q + 16, 512:1024])
+    send("t", lambda d: T.stt[:])
+    send("c1", lambda d: T.stc1[d])
 
     def ap(b):
         return T[b[0]][:, b[1]:b[2]]
 
-    def ts(out, in0, s1, s2, o0, o1=None, extra=(), qn="v"):
+    def ts(out, in0, s1, s2, o0, o1=None, extra=()):
         if o1 is None:
-            op(qn, [in0] + list(extra), [out], lambda e: e.tensor_scalar(ap(out), ap(in0), s1, None, o0))
+            op("v", [in0] + list(extra), [out], lambda e: e.tensor_scalar(ap(out), ap(in0), s1, None, o0))
         else:
-            op(qn, [in0] + list(extra), [out], lambda e: e.tensor_scalar(ap(out), ap(in0), s1, s2, o0, o1))
+            op("v", [in0] + list(extra), [out], lambda e: e.tensor_scalar(ap(out), ap(in0), s1, s2, o0, o1))
 
     def tt(out, in0, in1, o):
         op("v", [in0, in1], [out], lambda e: e.tensor_tensor(ap(out), ap(in0), ap(in1), o))
@@ -209,12 +202,12 @@ def rank_program(g, core, T, topo):
     def fill(out, c):
         op("v", [], [out], lambda e: e.memset(ap(out), c))
 
-    def act(out, in_, scale=1.0, bias=0.0):
-        op("a", [in_], [out], lambda e: e.activation(ap(out), ap(in_), AF.Identity, bias=bias, scale=scale))
+    def act(out, in_, scale=1.0, bias=0.0, extra=()):
+        op("a", [in_] + list(extra), [out], lambda e: e.activation(ap(out), ap(in_), AF.Identity, bias=bias, scale=scale))
 
-    def act_gather(out, win, lst, bias=0.0):
+    def act_gather(out, win, lst, bias=0.0, scale=1.0):
         op("a", [win, lst], [out],
-           lambda e: e.activation(ap(out), ap(win).indirect(ap(lst)), AF.Identity, bias=bias, scale=1.0))
+           lambda e: e.activation(ap(out), ap(win).indirect(ap(lst)), AF.Identity, bias=bias, scale=scale))
 
     def tt_gather(out, win, lst, in1, o):
         op("v", [win, lst, in1], [out], lambda e: e.tensor_tensor(ap(out), ap(win).indirect(ap(lst)), ap(in1), o))
@@ -234,26 +227,23 @@ def rank_program(g, core, T, topo):
     ts(("sm", 0, 8), ("cio", 0, 8), 16.0, pcol, A.mult, A.is_equal, extra=pfr)
     ts(("rc", 0, 80), ("cio", 0, 80), 16.0, c16, A.mult, A.add, extra=pfr)
     ts(("mj", 0, 128), ("mi", 0, 128), 31, None, A.bitwise_and)
-    ts(("mi", 0, 128), ("mi", 0, 128), 4, None, A.arith_shift_right)
     copy(("mf", 0, 128), ("mj", 0, 128))
-    copy(("mg", 0, 128), ("mi", 0, 128))
     ts(("nv", 0, 128), ("mf", 0, 128), -16.0, k255, A.mult, A.add, extra=pfr)
-    ts(("bones", 0, 128), ("mg", 0, 128), bcol, None, A.is_equal, extra=pfr)
     ts(("ni", 0, 128), ("eye", 0, 128), -2048.0, None, A.mult)
     for i in range(16):
         ts(("dsel", 128 * i, 128 * i + 128), ("eye", 0, 128), T.cm[:, i:i + 1], None, A.mult, extra=[("cm", 0, 16)])
-    for o in range(8):
-        ts(("selo", 128 * o, 128 * o + 128), ("ones", 0, 128), T.sm[:, o:o + 1], None, A.mult, extra=[("sm", 0, 8)])
     fill(("xl", R, XW), D)
     fill(("xh", R, XW), -1.0)
+    copy(("ru", 0, 320), ("ri", 0, 320))
+    ts(("mi", 0, 128), ("mi", 0, 128), 4, None, A.arith_shift_right)
+    copy(("mg", 0, 128), ("mi", 0, 128))
+    ts(("bones", 0, 128), ("mg", 0, 128), bcol, None, A.is_equal, extra=pfr)
     fill(("c96", 0, 512), float(CAP))
     fill(("pre", 7, 8), 0.0)
-
-    copy(("ru", 0, 320), ("ri", 0, 320))
     copy(("rf", 0, 320), ("ri", 0, 320))
+    tt(("rd", 0, 240), ("rf", 80, 320), ("rf", 0, 240), A.subtract)
     copy(("cu0", 0, 512), ("ci0", 0, 512))
     copy(("cf0", 0, 512), ("ci0", 0, 512))
-    tt(("rd", 0, 240), ("rf", 80, 320), ("rf", 0, 240), A.subtract)
 
     def extract(bank, ncol, buf, base, with_v):
         fns = []
@@ -275,81 +265,101 @@ def rank_program(g, core, T, topo):
         tt(("pp", 1024, 1536), ("pp", 512, 1024), ("s1", 512, 1024), o)
         tt(last, ("pp", 1024, 1536), ("s2", 0, 512), o)
 
-    def relayout(s, b, to, h, split):
-        for k in range(4):
-            o = 4 * h + k
+    def relayout(s, b, to, p, split):
+        for o in (2 * p, 2 * p + 1):
             for a in range(8):
-                qn = "a" if split and k % 2 else "s"
+                qn = "a" if split and o % 2 else "s"
                 dma(qn, s, [(b, 512 * o, 512 * o + 512)], [(to, 512 * a, 512 * a + 512)],
                     T[to][16 * o:16 * o + 16, 512 * a:512 * a + 512], T[b][16 * a:16 * a + 16, 512 * o:512 * o + 512])
 
     for t in range(RO):
         cu, cf = "cu%d" % t, "cf%d" % t
         lst = "ru" if t == 0 else "lq"
-        act_gather(("wr", 0, R), ("cio", 0, V), (lst, 0, 80))
-        for h in range(2):
-            for k in range(4):
-                b = 2048 * h + 512 * k
-                c = b // 16
-                j = 2 * h
-                act_gather(("wg", 2048 * j + 512 * k, 2048 * j + 512 * k + 512), ("wr", 0, R), (cu, c, c + 32), -(b + 255.0))
-                j, c = j + 1, c + 256
-                op("v", [("wr", 0, R), (cu, c, c + 32)], [("wg", 2048 * j + 512 * k, 2048 * j + 512 * k + 512)],
-                   lambda e, j=j, c=c, b=b, k=k: e.tensor_scalar(
-                       T.wg[:, 2048 * j + 512 * k:2048 * j + 512 * k + 512],
-                       T.wr[:, 0:R].indirect(T[cu][:, c:c + 32]), b + 255.0, None, A.subtract))
-        for j in range(4):
-            extract("z%d" % j, 128, "wg", 2048 * j, True)
-        if t == 0:
-            copy(("xl", 0, R), ("xs", 0, R))
-        else:
-            copy(("xs", 0, R), ("xl", 0, R))
+
+        def see(qn, j, k):
+            b = 2048 * (j // 2) + 512 * k
+            c = 256 * (j % 2) + b // 16
+            out, win, off = ("wg", 2048 * j + 512 * k, 2048 * j + 512 * k + 512), ("wr", 0, R), (cu, c, c + 32)
+            if qn == "a":
+                act_gather(out, win, off, -(b + 255.0))
+            else:
+                op("v", [win, off], [out],
+                   lambda e: e.tensor_scalar(ap(out), ap(win).indirect(ap(off)), b + 255.0, None, A.subtract))
 
         def lists(j):
             h, m = j // 2, j % 2
             tt(("tm", 128 * j, 128 * j + 128), ("z%d" % j, 0, 128), (cf, 256 * m + 128 * h, 256 * m + 128 * h + 128), A.max)
             ts(("off", 128 * j, 128 * j + 128), ("tm", 128 * j, 128 * j + 128), float(R), None, A.min)
 
-        def first(b, x, h):
-            act_gather((b, 2048 * h, 2048 * h + 2048), (x, 0, XW), ("off", 256 * h, 256 * h + 128))
+        def first(b, x, p):
+            c = 256 * (p // 2) + 64 * (p % 2)
+            act_gather((b, 1024 * p, 1024 * p + 1024), (x, 0, XW), ("off", c, c + 64))
 
-        def second(b, x, h, o):
-            tt_gather((b, 2048 * h, 2048 * h + 2048), (x, 0, XW), ("off", 256 * h + 128, 256 * h + 256),
-                      (b, 2048 * h, 2048 * h + 2048), o)
+        def second(b, x, p, o):
+            c = 256 * (p // 2) + 128 + 64 * (p % 2)
+            tt_gather((b, 1024 * p, 1024 * p + 1024), (x, 0, XW), ("off", c, c + 64), (b, 1024 * p, 1024 * p + 1024), o)
 
+        act_gather(("wr", 0, R), ("cio", 0, V), (lst, 0, 80))
+        for k in range(4):
+            see("a", 0, k)
+            see("v", 1, k)
+        extract("z0", 128, "wg", 0, True)
+        extract("z1", 128, "wg", 2048, True)
+        for k in range(4):
+            see("a", 2, k)
+        see("a", 3, 0)
+        extract("z2", 128, "wg", 4096, True)
+        if t == 0:
+            copy(("xl", 0, R), ("xs", 0, R))
+        see("v", 3, 1)
         lists(0)
         first("lo", "xl", 0)
-        lists(1)
-        lists(2)
+        see("v", 3, 2)
+        see("v", 3, 3)
+        extract("z3", 128, "wg", 6144, True)
         first("lo", "xl", 1)
-        act(("xh", 0, R), ("xl", 0, R))
-        first("hi", "xh", 0)
-        first("hi", "xh", 1)
-        act(("x5", 0, R), ("xl", 0, R), scale=1.25)
+        lists(1)
+
         second("lo", "xl", 0, A.min)
         relayout("rl%d" % t, "lo", "bl", 0, False)
-        lists(3)
+        lists(2)
         second("lo", "xl", 1, A.min)
         relayout("rl%d" % t, "lo", "bl", 1, False)
-        second("hi", "xh", 0, A.max)
-        relayout("rh%d" % t, "hi", "bh", 0, False)
-        second("hi", "xh", 1, A.max)
+        lists(3)
+        for p in (2, 3):
+            first("lo", "xl", p)
+            second("lo", "xl", p, A.min)
+            relayout("rl%d" % t, "lo", "bl", p, False)
+        act(("xh", 0, R), ("xl", 0, R))
+        for p in range(4):
+            first("hi", "xh", p)
+        for p in range(4):
+            second("hi", "xh", p, A.max)
+            if p < 3:
+                relayout("rh%d" % t, "hi", "bh", p, False)
         reduce_ranks("bl", A.min, ("lof", 0, 512))
-        relayout("rh%d" % t, "hi", "bh", 1, True)
+        relayout("rh%d" % t, "hi", "bh", 3, True)
+        act(("x5", 0, R), ("xl", 0, R), scale=1.25)
+        if t == 0:
+            dma("s", "get_t", [("ldt", 0, 8)], [("thi", 0, 1)], T.thi[:], T.ldt[:, 16 * q:16 * q + 16, :])
+            copy(("thf", 0, 1), ("thi", 0, 1))
+            for o in range(8):
+                ts(("selo", 128 * o, 128 * o + 128), ("cio", 0, 128), 0.0, T.sm[:, o:o + 1], A.is_ge, A.mult,
+                   extra=[("sm", 0, 8)])
+        else:
+            copy(("xs", 0, R), ("xl", 0, R))
         act(("fb", 0, 512), ("lof", 0, 512), scale=-0.25, bias=-0.375)
+        act(("lt", 0, 512), ("lof", 0, 512), bias=T.thf[:, 0:1], extra=[("thf", 0, 1)])
         for o in range(8):
             dma("s", "fs%d" % t, [("fb", 0, 512)], [("fd", 512 * o, 512 * o + 512)],
                 T.fd[:, 512 * o:512 * o + 512], T.fb[16 * o:16 * o + 16, :])
         for a in range(8):
             dma("s", "fg%d" % t, [("fd", 0, V)], [("ones", 0, V)], T.ones[16 * a:16 * a + 16, :], T.fd[:])
         if t == 0:
-            copy(("thf", 0, 1), ("thi", 0, 1))
-            copy(("cu1", 0, 512), ("ci1", 0, 512))
-            copy(("cf1", 0, 512), ("ci1", 0, 512))
+            dma("s", "get_c1", [("ldc1", 0, 8)], [("ci1", 0, 512)], T.ci1[:], T.ldc1[:])
         reduce_ranks("bh", A.max, ("pp", 1536, 2048))
 
-        tt(("df", 0, 512), ("pp", 1536, 2048), ("lof", 0, 512), A.subtract)
-        ts(("far", 0, 512), ("df", 0, 512), T.thf[:, 0:1], None, A.is_gt, extra=[("thf", 0, 1)])
+        tt(("far", 0, 512), ("pp", 1536, 2048), ("lt", 0, 512), A.is_gt)
         ops("t", [("bones", 0, 128), ("far", 0, 512)], [("z0", 0, 512)],
             [lambda e: e.matmul(T.z0[:], T.bones[:], T.far[:], True, True)])
         ts(("odd", 0, 512), ("z0", 0, 512), float(NEED), None, A.is_ge)
@@ -363,35 +373,39 @@ def rank_program(g, core, T, topo):
             act(("ft", 512 * o, 512 * o + 512), (z, 0, 512))
 
         for s in range(H):
-            act_gather(("fl", R * s, R * s + R), ("ft", 0, V), (lst, 80 * s, 80 * s + 80))
+            act_gather(("fl", R * s, R * s + R), ("ft", 0, V), (lst, 80 * s, 80 * s + 80), scale=-1.0 / 2048.0)
             extract("z%d" % s, 80, "fl", R * s, False)
         for s in range(H):
             tt_gather(("yb", 0, R), ("ones", 0, V), (lst, 80 * s, 80 * s + 80), ("x5", 0, R), A.add)
             ts(("xs", R * s + R, R * s + 2 * R), ("yb", 0, R), 0.0, float(TOP), A.max, A.min)
             if s < H - 1:
                 ts(("x5", 0, R), ("xs", R * s + R, R * s + 2 * R), 1.25, None, A.mult)
-        for s in range(H):
-            ts(("ef", 80 * s, 80 * s + 80), ("z%d" % s, 0, 80), -1024.0, None, A.is_lt)
-        e1, e2, e3 = ("ef", 0, 80), ("eg", 0, 80), ("eg", 80, 160)
-        tt(e2, e1, ("ef", 80, 160), A.mult)
-        tt(e3, e2, ("ef", 160, 240), A.mult)
-        tt(("k2", 0, 80), e1, e2, A.add)
+            if t == 0 and s == 0:
+                copy(("cu1", 0, 512), ("ci1", 0, 512))
+                copy(("cf1", 0, 512), ("ci1", 0, 512))
+        e1, e2, e3 = ("ef", 0, 80), ("ef", 80, 160), ("ef", 160, 240)
+        copy(e1, ("z0", 0, 80))
+        tt(e2, ("z1", 0, 80), e1, A.mult)
+        tt(e3, ("z2", 0, 80), e2, A.mult)
         if t == 0:
-            tt(("t1", 0, 80), e1, ("rd", 0, 80), A.mult)
-            tt(("t2", 0, 80), e2, ("rd", 80, 160), A.mult)
-            tt(("t3", 0, 80), e3, ("rd", 160, 240), A.mult)
-            tt(("t1", 0, 80), ("t1", 0, 80), ("rf", 0, 80), A.add)
-            tt(("t2", 0, 80), ("t2", 0, 80), ("t3", 0, 80), A.add)
+            tt(("eg", 0, 240), ("ef", 0, 240), ("rd", 0, 240), A.mult)
+            tt(("t1", 0, 80), ("eg", 0, 80), ("rf", 0, 80), A.add)
+            tt(("t2", 0, 80), ("eg", 80, 160), ("eg", 160, 240), A.add)
             tt(("lf", 0, 80), ("t1", 0, 80), ("t2", 0, 80), A.add)
             copy(("lq", 0, 80), ("lf", 0, 80))
+        tt(("k2", 0, 80), e1, e2, A.add)
         tt(("kk", 0, 80), ("k2", 0, 80), e3, A.add)
         ts(("t4", 0, 80), ("kk", 0, 80), float(R), None, A.mult)
         tt(("t4", 0, 80), ("t4", 0, 80), ("rc", 0, 80), A.add)
         copy(("so", 0, 80), ("t4", 0, 80))
-        to = ("xl", 0, R) if t == 0 else ("xf", 0, R)
-        op("v", [("xs", 0, 4 * R), ("so", 0, 80)], [to],
-           lambda e: e.tensor_copy(ap(to), T.xs[:].indirect(T.so[:])))
+
+        def pick(to, h):
+            op("v", [("xs", 0, 4 * R), ("so", 0, 80)], [(to, 640 * h, 640 * h + 640)],
+               lambda e: e.tensor_copy(T[to][:, 640 * h:640 * h + 640], T.xs[:].indirect(T.so[:, 40 * h:40 * h + 40])))
+
         if t == 0:
+            pick("xl", 0)
+            pick("xl", 1)
             tt(("t1", 0, 80), e1, ("rd", 80, 160), A.mult)
             tt(("t2", 0, 80), e2, ("rd", 160, 240), A.mult)
             tt(("t3", 0, 80), e1, ("rd", 160, 240), A.mult)
@@ -401,16 +415,22 @@ def rank_program(g, core, T, topo):
             copy(("lq", 80, 240), ("lf", 80, 240))
             copy(("cu", 0, 80), ("kk", 0, 80))
         else:
+            pick("xf", 0)
+            dma("s", "stg_y0", [("xf", 0, 640)], [("sty0", 0, 8)], T.sty0[:], T.xf[:, 0:640])
+            pick("xf", 1)
+            dma("a", "stg_y1", [("xf", 640, R)], [("sty1", 0, 8)], T.sty1[:], T.xf[:, 640:R])
             tt(("t1", 0, 80), ("cu", 0, 80), ("kk", 0, 80), A.add)
             ts(("cn", 0, 80), ("t1", 0, 80), 3.0, None, A.min)
 
-    dma("s", "stg_y", [("xf", 0, R)], [("sty", 0, 8)], T.sty[:], T.xf[:])
-    dma("a", "stg_c", [("cn", 0, 80)], [("stc", 0, 8)], T.stc[:], T.cn[:])
-    send("y", lambda d: T.sty[d])
+    dma("s", "stg_c", [("cn", 0, 80)], [("stc", 0, 8)], T.stc[:], T.cn[:])
+    send("y0", lambda d: T.sty0[d])
+    send("y1", lambda d: T.sty1[d])
     send("c", lambda d: T.stc[d])
-    dma("s", "own_y", [("sty", 0, 8)], [("ldy", q, q + 1)], T.ldy[q], T.sty[q])
+    dma("a", "own_y0", [("sty0", 0, 8)], [("ldy0", q, q + 1)], T.ldy0[q], T.sty0[q])
+    dma("a", "own_y1", [("sty1", 0, 8)], [("ldy1", q, q + 1)], T.ldy1[q], T.sty1[q])
     dma("a", "own_c", [("stc", 0, 8)], [("ldc", q, q + 1)], T.ldc[q], T.stc[q])
-    dma("s", "get_y", [("ldy", 0, 8)], [], T.yx[:], T.ldy[:])
+    dma("s", "get_y0", [("ldy0", 0, 8)], [], T.yx[:, 0:640], T.ldy0[:])
+    dma("s", "get_y1", [("ldy1", 0, 8)], [], T.yx[:, 640:R], T.ldy1[:])
     dma("a", "get_c", [("ldc", 0, 8)], [], T.yc[:], T.ldc[:])
     for s in total:
         need("g", s, total[s])

from concourse.bass import DstId, RemoteDMATransfer
from concourse.mybir import AluOpType, ActivationFunctionType

A = AluOpType
AF = ActivationFunctionType
V, R, RO, H, CAP, NEED = 4096, 1280, 2, 3, 96, 9
TOP = 2 ** 20 - 1
D = float(2 ** 21)
XW = R + 8

_S = {
    "ones": ([128, V], "float32"),
    "cio": ([128, V], "float32"),
    "wg": ([128, 4 * 2048], "bfloat16"),
    "lo": ([128, V], "float32"), "hi": ([128, V], "float32"),
    "bl": ([128, V], "float32"), "bh": ([128, V], "float32"),
    "xs": ([128, 4 * R], "int32"), "xl": ([128, XW], "float32"), "xh": ([128, XW], "float32"),
    "wr": ([128, R], "float32"), "fl": ([128, 3 * R], "bfloat16"), "ft": ([128, V], "bfloat16"),
    "yb": ([128, R], "float32"), "x5": ([128, R], "float32"), "xf": ([128, R], "float32"),
    "s1": ([128, 1024], "float32"), "s2": ([128, 512], "float32"),
    "lof": ([128, 512], "float32"), "lt": ([128, 512], "float32"), "odd": ([128, 512], "float32"),
    "pre": ([128, 520], "float32"), "c96": ([128, 512], "float32"),
    "far": ([128, 512], "bfloat16"), "cv": ([128, 512], "bfloat16"), "fb": ([128, 512], "float32"),
    "ci0": ([128, 512], "int32"), "ci1": ([128, 512], "int32"),
    "cf0": ([128, 512], "float32"), "cf1": ([128, 512], "float32"),
    "cu0": ([128, 512], "uint16"), "cu1": ([128, 512], "uint16"),
    "off": ([128, 512], "uint16"), "tm": ([128, 512], "float32"),
    "ri": ([128, 320], "int32"), "rf": ([128, 320], "float32"), "ru": ([128, 320], "uint16"),
    "rd": ([128, 240], "float32"), "lq": ([128, 240], "uint16"), "lf": ([128, 240], "float32"),
    "ef": ([128, 240], "float32"), "eg": ([128, 240], "float32"), "t1": ([128, 80], "float32"),
    "t2": ([128, 80], "float32"), "t3": ([128, 80], "float32"), "t4": ([128, 80], "float32"),
    "kk": ([128, 80], "float32"), "k2": ([128, 80], "float32"), "so": ([128, 80], "uint16"),
    "cu": ([128, 80], "float32"), "cn": ([128, 80], "float32"), "rc": ([128, 80], "float32"),
    "dsel": ([128, 16 * 128], "bfloat16"), "selo": ([128, 8 * 128], "bfloat16"),
    "bones": ([128, 128], "bfloat16"), "ni": ([128, 128], "bfloat16"), "nv": ([128, 128], "bfloat16"),
    "eye": ([128, 128], "float32"), "mi": ([128, 128], "int32"), "mj": ([128, 128], "int32"),
    "mf": ([128, 128], "float32"), "mg": ([128, 128], "float32"),
    "pi": ([128, 8], "int32"), "pf": ([128, 8], "float32"), "cm": ([128, 16], "float32"), "sm": ([128, 8], "float32"),
    "thi": ([128, 1], "int32"), "thf": ([128, 1], "float32"),
}
SCRATCH = {k: ("sbuf", s, d) for k, (s, d) in _S.items()}
for _k, _w, _d in (("c0", 64, "int32"), ("r", 40, "int32"), ("p", 160, "int32"), ("c1", 64, "int32"),
                   ("y0", 80, "float32"), ("y1", 80, "float32"), ("c", 10, "float32")):
    SCRATCH["st" + _k] = ("dram", [8, 128, _w], _d)
    SCRATCH["ld" + _k] = ("dram", [8, 128, _w], _d)
SCRATCH["stt"] = ("dram", [128, 1], "int32")
SCRATCH["ldt"] = ("dram", [8, 128, 1], "int32")
SCRATCH["fd"] = ("dram", [16, V], "float32")
SCRATCH["pp"] = ("psum", [128, 2048], "float32")
for _k in range(4):
    SCRATCH["z%d" % _k] = ("psum", [128, 512], "float32")
PSUM = ("pp", "z0", "z1", "z2", "z3")

CLASSES = ("c0", "r", "p", "t", "c1", "y0", "y1", "c")
TWO_CALLS = ("c0", "p", "c1", "y0", "y1", "r")
SEMAPHORES = (["q_v", "q_a", "q_t", "q_g", "sent"] + ["arr_" + k for k in CLASSES] + ["stg_" + k for k in CLASSES]
              + ["own_" + k for k in CLASSES] + ["get_" + k for k in CLASSES]
              + ["rl0", "rl1", "rh0", "rh1", "fs0", "fs1", "fg0", "fg1"])


def plan(core, cores, topo, two):
    r = cores.index(core)
    order = [cores[(r + k) % len(cores)] for k in range(1, len(cores))]
    near = [d for d in order if d in topo.cores_of(core)]
    far = [d for d in order if d not in near]
    fe = topo.engines(core, far[0])
    ne = [e for e in topo.engines(core, near[0]) if e not in fe]
    if two:
        first = [(d, fe[2 * k:2 * k + 2]) for k, d in enumerate(far[:4])]
        second = [(d, fe[4 * k:4 * k + 4]) for k, d in enumerate(far[4:])]
        return [second + [(near[0], ne)], first]
    return [[(d, fe[k:k + 1]) for k, d in enumerate(far)] + [(near[0], ne)]]


def rank_program(g, core, T, topo):
    q = T.rank_of(core)
    if q is None:
        return
    cores = list(T.cores)
    sem = T.sem
    queues = {"v": g.vector, "a": g.scalar, "t": g.tensor, "s": g.sync, "g": g}
    csem = {"v": "q_v", "a": "q_a", "t": "q_t", "g": "q_g"}
    total = {}
    known = {}
    closed = {}
    hist = {}

    def need(qn, s, val):
        if val is None:
            val = total[s]
            closed[s] = True
        if known.get((qn, s), 0) < val:
            queues[qn].wait_ge(sem[s], val)
            known[(qn, s)] = val

    def depend(qn, acc, own):
        wants = {}
        for name, lo, hi, w in acc:
            ps = name in PSUM
            if ps:
                lo, hi = lo // 512 * 512, -(-hi // 512) * 512
            for (l2, h2, w2, q2, s2, v2) in hist.get(name, []):
                if l2 >= hi or h2 <= lo or s2 == own:
                    continue
                if not (w or w2 or (ps and q2 != qn)):
                    continue
                v = total[s2] if v2 is None else v2
                if v2 is None:
                    closed[s2] = True
                wants[s2] = max(wants.get(s2, 0), v)
        for s in wants:
            need(qn, s, wants[s])

    def record(qn, acc, s, val):
        for name, lo, hi, w in acc:
            if name in PSUM:
                lo, hi = lo // 512 * 512, -(-hi // 512) * 512
            h = hist.setdefault(name, [])
            if w:
                h[:] = [e for e in h if not (e[0] >= lo and e[1] <= hi and not (e[4] == s and e[5] is None))]
            h.append((lo, hi, w, qn, s, val))

    def accs(rd, wr):
        return [(n, a, b, False) for n, a, b in rd] + [(n, a, b, True) for n, a, b in wr]

    def ops(qn, rd, wr, fns):
        s = csem[qn]
        acc = accs(rd, wr)
        depend(qn, acc, None)
        for f in fns[:-1]:
            f(queues[qn])
        fns[-1](queues[qn]).then_inc(sem[s], 1)
        total[s] = total.get(s, 0) + 1
        record(qn, acc, s, total[s])

    def op(qn, rd, wr, fn):
        ops(qn, rd, wr, [fn])

    def dma(qn, s, rd, wr, out, in_):
        assert s not in closed, s
        acc = accs(rd, wr)
        depend(qn, acc, s)
        queues[qn].dma_start(out=out, in_=in_).then_inc(sem[s], 16)
        total[s] = total.get(s, 0) + 16
        record(qn, acc, s, None)

    def send(c, piece):
        need("g", "stg_" + c, None)
        for call in plan(core, cores, topo, c in TWO_CALLS):
            tr = []
            for d, eng in call:
                rid, pid = topo.addr(d, core)
                m = sum(1 << e for e in eng)
                assert m & topo.mask(core, d) == m
                tr.append(RemoteDMATransfer(dst_ids=[DstId(rid=rid, pnc=pid)], dma_engine_mask=m,
                                            remote_sem=sem["arr_" + c], srcs=[piece(T.rank_of(d))], dsts=[T["ld" + c][q]]))
                total["sent"] = total.get("sent", 0) + len(eng)
            g.remote_dma_fused(tr, local_sem=sem.sent)
        n = 0
        for o in cores:
            if o != core:
                for call in plan(o, cores, topo, c in TWO_CALLS):
                    n += sum(len(eng) for d, eng in call if d == core)
        total["arr_" + c] = n
        record("far", [("ld" + c, 0, q, True), ("ld" + c, q + 1, 8, True)], "arr_" + c, n)

    dma("s", "stg_c0", [], [("stc0", 0, 8)], T.stc0[:], T.cand[:, 0:512])
    dma("a", "stg_r", [], [("str", 0, 8)], T["str"][:], T.ray[:])
    dma("s", "stg_p", [], [("stp", 0, 8)], T.stp[:], T.px[:])
    dma("a", "own_c0", [], [("ldc0", q, q + 1)], T.ldc0[q], T.cand[16 * q:16 * q + 16, 0:512])
    dma("a", "own_r", [], [("ldr", q, q + 1)], T.ldr[q], T.ray[16 * q:16 * q + 16, :])
    dma("s", "own_p", [], [("ldp", q, q + 1)], T.ldp[q], T.px[16 * q:16 * q + 16, :])
    op("g", [], [("pi", 0, 1)], lambda e: e.iota(T.pi[:, 0:1], [[0, 1]], 0, 1))
    send("r", lambda d: T["str"][d])
    send("c0", lambda d: T.stc0[d])
    send("p", lambda d: T.stp[d])
    dma("s", "get_r", [("ldr", 0, 8)], [("ri", 0, 320)], T.ri[:], T.ldr[:])
    dma("s", "get_c0", [("ldc0", 0, 8)], [("ci0", 0, 512)], T.ci0[:], T.ldc0[:])
    dma("s", "get_p", [("ldp", 0, 8)], [("xs", 0, R)], T.xs[:, 0:R], T.ldp[:])
    dma("s", "stg_t", [], [("stt", 0, 8)], T.stt[:], T.th[:])
    dma("s", "own_t", [], [("ldt", q, q + 1)], T.ldt[q], T.th[:])
    dma("s", "stg_c1", [], [("stc1", 0, 8)], T.stc1[:], T.cand[:, 512:1024])
    dma("s", "own_c1", [], [("ldc1", q, q + 1)], T.ldc1[q], T.cand[16 * q:16 * q + 16, 512:1024])
    send("t", lambda d: T.stt[:])
    send("c1", lambda d: T.stc1[d])

    def ap(b):
        return T[b[0]][:, b[1]:b[2]]

    def ts(out, in0, s1, s2, o0, o1=None, extra=()):
        if o1 is None:
            op("v", [in0] + list(extra), [out], lambda e: e.tensor_scalar(ap(out), ap(in0), s1, None, o0))
        else:
            op("v", [in0] + list(extra), [out], lambda e: e.tensor_scalar(ap(out), ap(in0), s1, s2, o0, o1))

    def tt(out, in0, in1, o):
        op("v", [in0, in1], [out], lambda e: e.tensor_tensor(ap(out), ap(in0), ap(in1), o))

    def copy(out, in_):
        op("v", [in_], [out], lambda e: e.tensor_copy(ap(out), ap(in_)))

    def fill(out, c):
        op("v", [], [out], lambda e: e.memset(ap(out), c))

    def act(out, in_, scale=1.0, bias=0.0, extra=()):
        op("a", [in_] + list(extra), [out], lambda e: e.activation(ap(out), ap(in_), AF.Identity, bias=bias, scale=scale))

    def act_gather(out, win, lst, bias=0.0, scale=1.0):
        op("a", [win, lst], [out],
           lambda e: e.activation(ap(out), ap(win).indirect(ap(lst)), AF.Identity, bias=bias, scale=scale))

    def tt_gather(out, win, lst, in1, o):
        op("v", [win, lst, in1], [out], lambda e: e.tensor_tensor(ap(out), ap(win).indirect(ap(lst)), ap(in1), o))

    fill(("ones", 0, V), 1.0)
    op("v", [("ones", 0, V)], [("cio", 0, V)],
       lambda e: e.tensor_tensor_scan(T.cio[:], T.ones[:], T.ones[:], -1.0, A.add, A.mult))
    ts(("pi", 1, 2), ("pi", 0, 1), 15, None, A.bitwise_and)
    ts(("pi", 2, 3), ("pi", 0, 1), 4, None, A.arith_shift_right)
    copy(("pf", 0, 3), ("pi", 0, 3))
    ts(("pf", 3, 4), ("pf", 1, 2), -1.0, 255.0, A.mult, A.add)
    pcol, c16, bcol, k255 = (T.pf[:, k:k + 1] for k in range(4))
    pfr = [("pf", 0, 4)]
    copy(("mi", 0, 128), ("cio", 0, 128))
    ts(("eye", 0, 128), ("cio", 0, 128), pcol, None, A.is_equal, extra=pfr)
    ts(("cm", 0, 16), ("cio", 0, 16), c16, -2048.0, A.is_equal, A.mult, extra=pfr)
    ts(("sm", 0, 8), ("cio", 0, 8), 16.0, pcol, A.mult, A.is_equal, extra=pfr)
    ts(("rc", 0, 80), ("cio", 0, 80), 16.0, c16, A.mult, A.add, extra=pfr)
    ts(("mj", 0, 128), ("mi", 0, 128), 31, None, A.bitwise_and)
    copy(("mf", 0, 128), ("mj", 0, 128))
    ts(("nv", 0, 128), ("mf", 0, 128), -16.0, k255, A.mult, A.add, extra=pfr)
    ts(("ni", 0, 128), ("eye", 0, 128), -2048.0, None, A.mult)
    for i in range(16):
        ts(("dsel", 128 * i, 128 * i + 128), ("eye", 0, 128), T.cm[:, i:i + 1], None, A.mult, extra=[("cm", 0, 16)])
    fill(("xl", R, XW), D)
    fill(("xh", R, XW), -1.0)
    copy(("ru", 0, 320), ("ri", 0, 320))
    ts(("mi", 0, 128), ("mi", 0, 128), 4, None, A.arith_shift_right)
    copy(("mg", 0, 128), ("mi", 0, 128))
    ts(("bones", 0, 128), ("mg", 0, 128), bcol, None, A.is_equal, extra=pfr)
    fill(("c96", 0, 512), float(CAP))
    fill(("pre", 7, 8), 0.0)
    copy(("rf", 0, 320), ("ri", 0, 320))
    tt(("rd", 0, 240), ("rf", 80, 320), ("rf", 0, 240), A.subtract)
    copy(("cu0", 0, 512), ("ci0", 0, 512))
    copy(("cf0", 0, 512), ("ci0", 0, 512))

    def extract(bank, ncol, buf, base, with_v):
        fns = []
        for i in range(16):
            fns.append(lambda e, i=i: e.matmul(T[bank][:, 0:ncol], T.dsel[:, 128 * i:128 * i + 128],
                                               T[buf][:, base + i:base + 16 * ncol:16], i == 0, (not with_v) and i == 15))
        rd = [("dsel", 0, 2048), (buf, base, base + 16 * ncol)]
        if with_v:
            fns.append(lambda e: e.matmul(T[bank][:, 0:ncol], T.ni[:], T.nv[:, 0:ncol], False, True))
            rd += [("ni", 0, 128), ("nv", 0, 128)]
        ops("t", rd, [(bank, 0, 512)], fns)

    def reduce_ranks(b, o, last):
        act(("pp", 0, 1024), (b, 0, 1024))
        act(("pp", 1024, 2048), (b, 1024, 2048))
        tt(("s1", 0, 1024), ("pp", 0, 1024), (b, 2048, 3072), o)
        tt(("pp", 0, 1024), ("pp", 1024, 2048), (b, 3072, 4096), o)
        tt(("s2", 0, 512), ("pp", 0, 512), ("s1", 0, 512), o)
        tt(("pp", 1024, 1536), ("pp", 512, 1024), ("s1", 512, 1024), o)
        tt(last, ("pp", 1024, 1536), ("s2", 0, 512), o)

    def relayout(s, b, to, p, split):
        for o in (2 * p, 2 * p + 1):
            for a in range(8):
                qn = "a" if split and o % 2 else "s"
                dma(qn, s, [(b, 512 * o, 512 * o + 512)], [(to, 512 * a, 512 * a + 512)],
                    T[to][16 * o:16 * o + 16, 512 * a:512 * a + 512], T[b][16 * a:16 * a + 16, 512 * o:512 * o + 512])

    for t in range(RO):
        cu, cf = "cu%d" % t, "cf%d" % t
        lst = "ru" if t == 0 else "lq"

        def see(qn, j, k):
            b = 2048 * (j // 2) + 512 * k
            c = 256 * (j % 2) + b // 16
            out, win, off = ("wg", 2048 * j + 512 * k, 2048 * j + 512 * k + 512), ("wr", 0, R), (cu, c, c + 32)
            if qn == "a":
                act_gather(out, win, off, -(b + 255.0))
            else:
                op("v", [win, off], [out],
                   lambda e: e.tensor_scalar(ap(out), ap(win).indirect(ap(off)), b + 255.0, None, A.subtract))

        def lists(j):
            h, m = j // 2, j % 2
            tt(("tm", 128 * j, 128 * j + 128), ("z%d" % j, 0, 128), (cf, 256 * m + 128 * h, 256 * m + 128 * h + 128), A.max)
            ts(("off", 128 * j, 128 * j + 128), ("tm", 128 * j, 128 * j + 128), float(R), None, A.min)

        def first(b, x, p):
            c = 256 * (p // 2) + 64 * (p % 2)
            act_gather((b, 1024 * p, 1024 * p + 1024), (x, 0, XW), ("off", c, c + 64))

        def second(b, x, p, o):
            c = 256 * (p // 2) + 128 + 64 * (p % 2)
            tt_gather((b, 1024 * p, 1024 * p + 1024), (x, 0, XW), ("off", c, c + 64), (b, 1024 * p, 1024 * p + 1024), o)

        act_gather(("wr", 0, R), ("cio", 0, V), (lst, 0, 80))
        for k in range(4):
            see("a", 0, k)
            see("v", 1, k)
        extract("z0", 128, "wg", 0, True)
        extract("z1", 128, "wg", 2048, True)
        for k in range(4):
            see("a", 2, k)
        see("a", 3, 0)
        extract("z2", 128, "wg", 4096, True)
        if t == 0:
            copy(("xl", 0, R), ("xs", 0, R))
        see("v", 3, 1)
        lists(0)
        first("lo", "xl", 0)
        see("v", 3, 2)
        see("v", 3, 3)
        extract("z3", 128, "wg", 6144, True)
        first("lo", "xl", 1)
        lists(1)

        second("lo", "xl", 0, A.min)
        relayout("rl%d" % t, "lo", "bl", 0, False)
        lists(2)
        second("lo", "xl", 1, A.min)
        relayout("rl%d" % t, "lo", "bl", 1, False)
        lists(3)
        for p in (2, 3):
            first("lo", "xl", p)
            second("lo", "xl", p, A.min)
            relayout("rl%d" % t, "lo", "bl", p, False)
        act(("xh", 0, R), ("xl", 0, R))
        for p in range(4):
            first("hi", "xh", p)
        for p in range(4):
            second("hi", "xh", p, A.max)
            if p < 3:
                relayout("rh%d" % t, "hi", "bh", p, False)
        reduce_ranks("bl", A.min, ("lof", 0, 512))
        relayout("rh%d" % t, "hi", "bh", 3, True)
        act(("x5", 0, R), ("xl", 0, R), scale=1.25)
        if t == 0:
            dma("s", "get_t", [("ldt", 0, 8)], [("thi", 0, 1)], T.thi[:], T.ldt[:, 16 * q:16 * q + 16, :])
            copy(("thf", 0, 1), ("thi", 0, 1))
            for o in range(8):
                ts(("selo", 128 * o, 128 * o + 128), ("cio", 0, 128), 0.0, T.sm[:, o:o + 1], A.is_ge, A.mult,
                   extra=[("sm", 0, 8)])
        else:
            copy(("xs", 0, R), ("xl", 0, R))
        act(("fb", 0, 512), ("lof", 0, 512), scale=-0.25, bias=-0.375)
        act(("lt", 0, 512), ("lof", 0, 512), bias=T.thf[:, 0:1], extra=[("thf", 0, 1)])
        for o in range(8):
            dma("s", "fs%d" % t, [("fb", 0, 512)], [("fd", 512 * o, 512 * o + 512)],
                T.fd[:, 512 * o:512 * o + 512], T.fb[16 * o:16 * o + 16, :])
        for a in range(8):
            dma("s", "fg%d" % t, [("fd", 0, V)], [("ones", 0, V)], T.ones[16 * a:16 * a + 16, :], T.fd[:])
        if t == 0:
            dma("s", "get_c1", [("ldc1", 0, 8)], [("ci1", 0, 512)], T.ci1[:], T.ldc1[:])
        reduce_ranks("bh", A.max, ("pp", 1536, 2048))

        tt(("far", 0, 512), ("pp", 1536, 2048), ("lt", 0, 512), A.is_gt)
        ops("t", [("bones", 0, 128), ("far", 0, 512)], [("z0", 0, 512)],
            [lambda e: e.matmul(T.z0[:], T.bones[:], T.far[:], True, True)])
        ts(("odd", 0, 512), ("z0", 0, 512), float(NEED), None, A.is_ge)
        op("v", [("odd", 0, 512), ("c96", 0, 512)], [("pre", 8, 520)],
           lambda e: e.tensor_tensor_scan(T.pre[:, 8:520], T.odd[:], T.c96[:], 0.0, A.add, A.min))
        tt(("cv", 0, 512), ("pre", 8, 520), ("pre", 7, 519), A.subtract)
        for o in range(8):
            z = "z%d" % (o % 4)
            ops("t", [("selo", 128 * o, 128 * o + 128), ("cv", 0, 512)], [(z, 0, 512)],
                [lambda e, z=z, o=o: e.matmul(T[z][:], T.selo[:, 128 * o:128 * o + 128], T.cv[:], True, True)])
            act(("ft", 512 * o, 512 * o + 512), (z, 0, 512))

        for s in range(H):
            act_gather(("fl", R * s, R * s + R), ("ft", 0, V), (lst, 80 * s, 80 * s + 80), scale=-1.0 / 2048.0)
            extract("z%d" % s, 80, "fl", R * s, False)
        for s in range(H):
            tt_gather(("yb", 0, R), ("ones", 0, V), (lst, 80 * s, 80 * s + 80), ("x5", 0, R), A.add)
            ts(("xs", R * s + R, R * s + 2 * R), ("yb", 0, R), 0.0, float(TOP), A.max, A.min)
            if s < H - 1:
                ts(("x5", 0, R), ("xs", R * s + R, R * s + 2 * R), 1.25, None, A.mult)
            if t == 0 and s == 0:
                copy(("cu1", 0, 512), ("ci1", 0, 512))
                copy(("cf1", 0, 512), ("ci1", 0, 512))
        e1, e2, e3 = ("ef", 0, 80), ("ef", 80, 160), ("ef", 160, 240)
        copy(e1, ("z0", 0, 80))
        tt(e2, ("z1", 0, 80), e1, A.mult)
        tt(e3, ("z2", 0, 80), e2, A.mult)
        if t == 0:
            tt(("eg", 0, 240), ("ef", 0, 240), ("rd", 0, 240), A.mult)
            tt(("t1", 0, 80), ("eg", 0, 80), ("rf", 0, 80), A.add)
            tt(("t2", 0, 80), ("eg", 80, 160), ("eg", 160, 240), A.add)
            tt(("lf", 0, 80), ("t1", 0, 80), ("t2", 0, 80), A.add)
            copy(("lq", 0, 80), ("lf", 0, 80))
        tt(("k2", 0, 80), e1, e2, A.add)
        tt(("kk", 0, 80), ("k2", 0, 80), e3, A.add)
        ts(("t4", 0, 80), ("kk", 0, 80), float(R), None, A.mult)
        tt(("t4", 0, 80), ("t4", 0, 80), ("rc", 0, 80), A.add)
        copy(("so", 0, 80), ("t4", 0, 80))

        def pick(to, h):
            op("v", [("xs", 0, 4 * R), ("so", 0, 80)], [(to, 640 * h, 640 * h + 640)],
               lambda e: e.tensor_copy(T[to][:, 640 * h:640 * h + 640], T.xs[:].indirect(T.so[:, 40 * h:40 * h + 40])))

        if t == 0:
            pick("xl", 0)
            pick("xl", 1)
            tt(("t1", 0, 80), e1, ("rd", 80, 160), A.mult)
            tt(("t2", 0, 80), e2, ("rd", 160, 240), A.mult)
            tt(("t3", 0, 80), e1, ("rd", 160, 240), A.mult)
            tt(("t1", 0, 80), ("t1", 0, 80), ("rf", 80, 160), A.add)
            tt(("lf", 80, 160), ("t1", 0, 80), ("t2", 0, 80), A.add)
            tt(("lf", 160, 240), ("t3", 0, 80), ("rf", 160, 240), A.add)
            copy(("lq", 80, 240), ("lf", 80, 240))
            copy(("cu", 0, 80), ("kk", 0, 80))
        else:
            pick("xf", 0)
            dma("s", "stg_y0", [("xf", 0, 640)], [("sty0", 0, 8)], T.sty0[:], T.xf[:, 0:640])
            pick("xf", 1)
            dma("a", "stg_y1", [("xf", 640, R)], [("sty1", 0, 8)], T.sty1[:], T.xf[:, 640:R])
            tt(("t1", 0, 80), ("cu", 0, 80), ("kk", 0, 80), A.add)
            ts(("cn", 0, 80), ("t1", 0, 80), 3.0, None, A.min)

    dma("s", "stg_c", [("cn", 0, 80)], [("stc", 0, 8)], T.stc[:], T.cn[:])
    send("y0", lambda d: T.sty0[d])
    send("y1", lambda d: T.sty1[d])
    send("c", lambda d: T.stc[d])
    dma("a", "own_y0", [("sty0", 0, 8)], [("ldy0", q, q + 1)], T.ldy0[q], T.sty0[q])
    dma("a", "own_y1", [("sty1", 0, 8)], [("ldy1", q, q + 1)], T.ldy1[q], T.sty1[q])
    dma("a", "own_c", [("stc", 0, 8)], [("ldc", q, q + 1)], T.ldc[q], T.stc[q])
    dma("s", "get_y0", [("ldy0", 0, 8)], [], T.yx[:, 0:640], T.ldy0[:])
    dma("s", "get_y1", [("ldy1", 0, 8)], [], T.yx[:, 640:R], T.ldy1[:])
    dma("a", "get_c", [("ldc", 0, 8)], [], T.yc[:], T.ldc[:])
    for s in total:
        need("g", s, total[s])
